import numpy as np
import ml_dtypes


def mxq(x, axis, fmt="e4m3"):
    dtype, down = {"e4m3": (ml_dtypes.float8_e4m3fn, 7), "e5m2": (ml_dtypes.float8_e5m2, 14)}[fmt]
    v = np.moveaxis(np.asarray(x, np.float32).astype(ml_dtypes.bfloat16).astype(np.float64), axis, -1)
    blocks = v.reshape(v.shape[:-1] + (-1, 32))
    amax = np.abs(blocks).max(-1, keepdims=True)
    byte = np.maximum(np.where(amax > 0, np.frexp(amax)[1] - 1 + 127, 0) - down, 1)
    scale = np.exp2(byte - 127.0)
    codes = (blocks / scale).astype(np.float32).astype(dtype).astype(np.float64)
    return np.moveaxis((codes * scale).reshape(v.shape), -1, axis)


WIDE = False


def mx_kscale(k):
    if not WIDE:
        return np.ones(k)
    levels = np.array([10, -10, 5, -5, 0])
    if k % 512:
        return np.exp2(np.random.permutation(np.resize(levels, k // 32))).repeat(32)
    a = np.empty((k // 512, 16))
    for p in range(k // 512):
        a[p, :8] = np.random.permutation(np.resize(levels, 8))
        for g in range(8):
            far = levels[np.abs(levels - a[p, g]) >= 10]
            a[p, g + 8] = far[np.random.randint(len(far))]
    return np.exp2(a.ravel()).repeat(32)


def f64(x):
    return np.asarray(x).astype(np.float64)


def striped(idx):
    return np.tile(idx.reshape(-1, 16).T, (8, 1)).astype(np.uint16)


def unstriped(offs):
    return offs[:16].T.reshape(-1).astype(np.int64)


E2M1 = np.array([0.0, 0.5, 1.0, 1.5, 2.0, 3.0, 4.0, 6.0, -0.0, -0.5, -1.0, -1.5, -2.0, -3.0, -4.0, -6.0])


def pack_weight(w, fmt):
    k, n = w.shape
    w = f64(np.asarray(w, np.float32).astype(ml_dtypes.bfloat16)).reshape(k // 32, 32, n)
    amax = np.abs(w).max(1)
    if fmt == "e4m3":
        byte = np.frexp(amax)[1] - 1 + 127 - 7
    else:
        mant, ex = np.frexp(amax / 6.0)
        byte = np.where(mant > 0.5, ex, ex - 1) + 127
    byte = np.clip(np.where(amax > 0, byte, 1), 1, 254)
    scaled = (w * np.exp2(127.0 - byte)[:, None, :]).reshape(k, n).astype(np.float32)
    by_word = np.ascontiguousarray(scaled.reshape(k // 512, 128, 4, n).transpose(0, 1, 3, 2))
    if fmt == "e4m3":
        words = by_word.astype(ml_dtypes.float8_e4m3fn).view(np.uint8)
    else:
        c = by_word.astype(ml_dtypes.float4_e2m1fn).view(np.uint8) & 0xF
        words = (c[..., 0::2] | (c[..., 1::2] << 4)).reshape(k // 512, 128, 2 * n)
    return np.ascontiguousarray(words), np.ascontiguousarray(byte.astype(np.uint8).reshape(k // 512, 16, n))


def unpack_weight(words, scales, fmt):
    g, _, n = scales.shape
    words = np.ascontiguousarray(words).reshape(g, 128, n, -1)
    if fmt == "e4m3":
        vals = words.view(ml_dtypes.float8_e4m3fn).astype(np.float64)
    else:
        nib = np.empty((g, 128, n, 4), np.uint8)
        nib[..., 0::2] = words & 0xF
        nib[..., 1::2] = words >> 4
        vals = E2M1[nib]
    vals = vals * np.repeat(np.exp2(scales.astype(np.float64) - 127.0), 8, axis=1)[..., None]
    return vals.transpose(0, 1, 3, 2).reshape(g * 512, n)


def gelu(v):
    return 0.5 * v * (1.0 + np.tanh(np.sqrt(2.0 / np.pi) * (v + 0.044715 * v**3)))


def bf(x):
    return np.asarray(x, np.float32).astype(ml_dtypes.bfloat16)


def planes(Y):
    n, m = Y.shape
    b = f64(bf(Y)).reshape(n // 32, 32, m)
    amax = np.abs(b).max(1)
    byte = np.clip(np.where(amax > 0, np.frexp(amax)[1] - 1 + 127 - 7, 1), 1, 254)
    codes = (b * np.exp2(127.0 - byte)[:, None, :]).reshape(n, m).astype(np.float32).astype(ml_dtypes.float8_e4m3fn).view(np.uint8)
    words = codes.reshape(n // 512, 128, 4, m).transpose(0, 1, 3, 2)
    return np.ascontiguousarray(words), np.ascontiguousarray(byte.astype(np.uint8).reshape(n // 512, 16, m))


K, T, S, H, T2, P, N = 1024, 2048, 1024, 512, 2048, 1024, 1024

def setup_inputs():
    n = np.random.standard_normal
    s = mx_kscale(K)[:, None]
    u = mx_kscale(H)[:, None]
    tab_words, tab_scales = pack_weight(n((K, T)) * s, "e4m3")
    w2_words, w2_scales = pack_weight(0.8 * n((H, N)) / np.sqrt(H) / u, "e2m1")
    return {
        "tab_words": tab_words, "tab_scales": tab_scales,
        "offs": striped(np.random.permutation(T)[:S]),
        "offs2": striped(np.random.permutation(T2)[:S]),
        "offs3": striped(np.random.permutation(T2)[:P]),
        "w1": (n((K, H)) / np.sqrt(K) / s * u.T).astype(np.float32),
        "page0": (n((H, T2)) * u).astype(np.float32),
        "w2_words": w2_words, "w2_scales": w2_scales,
        "w3": (0.8 * n((H, N)) / np.sqrt(H) / u).astype(np.float32),
        "gain": np.exp(0.8 * n(N)).astype(np.float32),
    }

def reference(tab_words, tab_scales, offs, offs2, offs3, w1, page0, w2_words, w2_scales, w3, gain):
    v = unpack_weight(tab_words, tab_scales, "e4m3")[:, unstriped(offs)]
    h = mxq(f64(w1), 0, "e4m3").T @ v
    page = f64(page0).copy()
    l2 = unstriped(offs2)
    page[:, l2] = page[:, l2] + h
    x = page[:, unstriped(offs3)]
    ax = np.abs(x)
    w2 = unpack_weight(w2_words, w2_scales, "e2m1")
    y = w2.T @ mxq(x, 0, "e4m3") + mxq(f64(w3), 0, "e4m3").T @ mxq(ax, 0, "e4m3")
    y = np.tanh(y) * f64(gain)[:, None]
    words, scales = planes(y)
    return y, words, scales

from contextlib import ExitStack

import concourse.mybir as mybir

K, T, S, H, T2, M, N = 1024, 2048, 1024, 512, 2048, 1024, 1024
FLOPS = 2 * K * H * S + 2 * 2 * H * N * M

F32 = mybir.dt.float32
BF16 = mybir.dt.bfloat16
I32 = mybir.dt.int32
U32 = mybir.dt.uint32
U16 = mybir.dt.uint16
U8 = mybir.dt.uint8
FP8X4 = mybir.dt.float8_e4m3fn_x4
FP4X4 = mybir.dt.float4_e2m1fn_x4
ALU = mybir.AluOpType
ACT = mybir.ActivationFunctionType

P = 128
PACK = 4
PASS = P * PACK
BANK = 512
CHUNK = 256
CHUNKS = M // CHUNK
PASSES = K // PASS
GROUPS = N // PASS
QUADS = 4
ABS_ON_SCALAR = 1


def tile_list_fuel_dryness_page_kernel(
    tc, tab_words, tab_scales, offs, offs2, offs3, w1, page0, w2_words, w2_scales, w3, gain, out_0, out_1, out_2
):
    nc = tc.nc
    with ExitStack() as ctx:
        sb = ctx.enter_context(tc.tile_pool(name="sb", bufs=1))
        psum = ctx.enter_context(tc.psum_pool(name="psum", bufs=8))

        def tile(name, shape, dtype, tag=None, bufs=1):
            return sb.tile(shape, dtype, name=name, tag=tag or name, bufs=bufs, align_bytes=64)

        list1 = tile("list1", [P, S // 16], U16)
        list2 = tile("list2", [P, S // 16], U16)
        list3 = tile("list3", [P, M // 16], U16)
        tab = [tile(f"tab{a}", [P, T], I32) for a in range(PASSES)]
        tab_sc = tile("tab_sc", [P, T], U8)
        w1_raw = [tile(f"w1_raw{a}", [P, PACK * H], F32) for a in range(PASSES)]
        w2_raw = tile("w2_raw", [P, 2 * N], U8)
        w2_sc_raw = tile("w2_sc_raw", [P, N], U8)
        w3_raw = [tile(f"w3_raw{g}", [P, PACK * PASS], F32, f"w1_raw{g}") for g in range(GROUPS)]
        page = [tile(f"page{t}", [P, T2], F32) for t in range(PACK)]
        gains = tile("gains", [P, GROUPS * PACK], F32)

        nc.vector.memset(tab_sc[:].bitcast(I32), 0)
        nc.gpsimd.memset(w2_sc_raw[:].bitcast(I32), 0)

        def load_tab(a):
            nc.sync.dma_start(out=tab[a][:], in_=tab_words[a].rearrange("p t i -> p (t i)").bitcast(I32))

        def load_w1(a):
            nc.sync.dma_start(out=w1_raw[a][:], in_=w1[a * PASS : (a + 1) * PASS, :].rearrange("(p i) r -> p (i r)", i=PACK))

        def load_page(t):
            nc.sync.dma_start(out=page[t][:], in_=page0.rearrange("(p t) c -> t p c", t=PACK)[t])

        def load_w3(g):
            nc.sync.dma_start(
                out=w3_raw[g][:].rearrange("p (i n) -> p i n", i=PACK),
                in_=w3.rearrange("(p i) n -> p i n", i=PACK)[:, :, g * PASS : (g + 1) * PASS],
            )

        nc.sync.dma_start(out=list1[:], in_=offs)
        load_tab(0)
        for q in range(QUADS):
            nc.sync.dma_start(
                out=tab_sc[32 * q : 32 * q + 4 * PASSES, :].bitcast(I32),
                in_=tab_scales[:, 4 * q : 4 * q + 4, :].bitcast(I32),
            )
        nc.sync.dma_start(out=w2_raw[:].bitcast(I32), in_=w2_words[0].bitcast(I32))
        load_tab(1)
        for q in range(QUADS):
            nc.sync.dma_start(
                out=w2_sc_raw[32 * q : 32 * q + 4, :].bitcast(I32), in_=w2_scales[0, 4 * q : 4 * q + 4, :].bitcast(I32)
            )
        nc.sync.dma_start(out=list2[:], in_=offs2)
        load_page(0)
        load_w1(0)
        load_page(1)
        load_page(2)
        load_w1(1)
        load_page(3)
        nc.sync.dma_start(out=list3[:], in_=offs3)
        load_w3(0)
        load_w3(1)
        nc.sync.dma_start(
            out=gains[:].rearrange("p (g t) -> p g t", t=PACK), in_=gain.rearrange("(g p t) -> p g t", p=P, t=PACK)
        )

        def quantize(name, rounded, tag=None, bufs=1):
            cols = rounded.shape[1] // PACK
            codes = tile(name + "_codes", [P, cols], U32, tag and tag + "_codes", bufs)
            scales = tile(name + "_scales", [P, cols], U8, tag and tag + "_scales", bufs)
            nc.vector.quantize_mx(out=codes[:].bitcast(FP8X4), scales=scales[:], in_=rounded[:])
            return codes, scales

        def round_weight(name, raw):
            rounded = tile(name, [P, PACK * PASS], BF16)
            nc.scalar.copy(
                out=rounded[:].rearrange("p (t q i) -> p q i t", t=PACK, i=PACK),
                in_=raw[:].rearrange("p (i q t) -> p q i t", i=PACK, t=PACK),
            )
            return rounded

        def woven(rounded, planes):
            return (
                rounded[:].rearrange("p (c i t) -> p c t i", i=4, t=PACK),
                planes[:].rearrange("p (t c i) -> p c t i", t=PACK, i=4),
            )

        v = [tile(f"v{a}", [P, S], U32) for a in range(PASSES)]
        v_sc = tile("v_sc", [P, S], U8)
        nc.vector.tensor_copy(out=v[0][:], in_=tab[0][:].bitcast(U32).indirect(list1[:]))
        nc.vector.tensor_copy(out=v_sc[:], in_=tab_sc[:].indirect(list1[:]))
        w1_bf = [round_weight(f"w1_bf{a}", w1_raw[a]) for a in range(PASSES)]

        w2 = tile("w2", [P, 2 * N], U8)
        w2_sc = tile("w2_sc", [P, N], U8)
        nc.vector.tensor_copy(
            out=w2[:].bitcast(U16).rearrange("p (g t q) -> p g q t", g=GROUPS, t=PACK),
            in_=w2_raw[:].bitcast(U16).rearrange("p (g q t) -> p g q t", g=GROUPS, t=PACK),
        )
        nc.vector.tensor_copy(
            out=w2_sc[:].rearrange("p (g t q) -> p g q t", g=GROUPS, t=PACK),
            in_=w2_sc_raw[:].rearrange("p (g q t) -> p g q t", g=GROUPS, t=PACK),
        )
        nc.vector.tensor_copy(out=v[1][:], in_=tab[1][:].bitcast(U32).indirect(list1[:]))
        old = []
        w1_q = []
        for t in range(PACK):
            old.append(tile(f"old{t}", [P, S], F32))
            if t % 2:
                w1_q.append(quantize(f"w1_{t // 2}", w1_bf[t // 2]))
            nc.vector.tensor_copy(out=old[t][:], in_=page[t][:].indirect(list2[:]))

        h = [tile(f"h{t}", [P, S], F32) for t in range(PACK)]
        banks = [psum.tile([P, BANK], F32, name="bank", tag="bank") for b in range(PACK * S // BANK)]
        for a in range(PASSES):
            for b, bank in enumerate(banks):
                t, j0 = divmod(b * BANK, S)
                rows = slice(t * P, (t + 1) * P)
                cols = slice(j0, j0 + BANK)
                nc.tensor.matmul_mx(
                    out=bank[:],
                    lhsT=w1_q[a][0][:, rows].bitcast(FP8X4),
                    lhsT_scale=w1_q[a][1][:, rows],
                    rhs=v[a][:, cols].bitcast(FP8X4),
                    rhs_scale=v_sc[4 * a : P, cols],
                    start=(a == 0),
                    stop=(a == PASSES - 1),
                )
                if a == PASSES - 1:
                    nc.scalar.copy(out=h[t][:, cols], in_=bank[:])
        w3_bf = [round_weight(f"w3_bf{g}", w3_raw[g]) for g in range(GROUPS)]

        def fetch_x(x_planes, c, t):
            per = CHUNK // 16
            nc.vector.tensor_copy(
                out=x_planes[:, t * CHUNK : (t + 1) * CHUNK], in_=page[t][:].indirect(list3[:, c * per : (c + 1) * per])
            )

        x_first = tile("x_first", [P, PACK * CHUNK], F32, "x_even")
        for t in range(PACK):
            nc.vector.tensor_tensor(out=page[t][:].indirect(list2[:]), in0=old[t][:], in1=h[t][:], op=ALU.add)
            if t > 0:
                fetch_x(x_first, 0, t - 1)
        w3_q = [quantize(f"w3_{g}", w3_bf[g]) for g in range(GROUPS)]

        y_codes = [tile(f"y_codes{g}", [P, M], U32) for g in range(GROUPS)]
        y_scales = tile("y_scales", [P, GROUPS * M], U8)

        def make_x(c):
            if c == 0:
                x_planes = x_first
                fetch_x(x_planes, c, PACK - 1)
            else:
                x_planes = tile(f"x_planes{c}", [P, PACK * CHUNK], F32, "x_odd" if c % 2 else "x_even")
                for t in range(PACK):
                    fetch_x(x_planes, c, t)
            x_bf = tile(f"x_bf{c}", [P, PACK * CHUNK], BF16)
            ax_bf = tile(f"ax_bf{c}", [P, PACK * CHUNK], BF16, "x_odd" if c == 0 else None)
            dst, src = woven(x_bf, x_planes)
            nc.vector.tensor_copy(out=dst, in_=src)
            if c < ABS_ON_SCALAR:
                dst, src = woven(ax_bf, x_planes)
                nc.scalar.activation(out=dst, in_=src, func=ACT.Abs)
            else:
                nc.vector.scalar_tensor_tensor(
                    out=ax_bf[:], in0=x_bf[:], scalar=-1.0, in1=x_bf[:], op0=ALU.mult, op1=ALU.max
                )
            return quantize(f"x{c}", x_bf), quantize(f"ax{c}", ax_bf)

        def make_y(c, g, x_q, ax_q):
            y = tile(f"y{c}_{g}", [P, PACK * CHUNK], F32)
            per_bank = BANK // CHUNK
            for t0 in range(0, PACK, per_bank):
                bank = psum.tile([P, BANK], F32, name="bank", tag="bank")
                for t in range(t0, t0 + per_bank):
                    n0 = g * PASS + t * P
                    nc.tensor.matmul_mx(
                        out=bank[:, (t - t0) * CHUNK : (t - t0 + 1) * CHUNK],
                        lhsT=w2[:, 2 * n0 : 2 * (n0 + P)].bitcast(FP4X4),
                        lhsT_scale=w2_sc[:, n0 : n0 + P],
                        rhs=x_q[0][:].bitcast(FP8X4),
                        rhs_scale=x_q[1][:],
                        start=(t == t0),
                        stop=False,
                    )
                for t in range(t0, t0 + per_bank):
                    nc.tensor.matmul_mx(
                        out=bank[:, (t - t0) * CHUNK : (t - t0 + 1) * CHUNK],
                        lhsT=w3_q[g][0][:, t * P : (t + 1) * P].bitcast(FP8X4),
                        lhsT_scale=w3_q[g][1][:, t * P : (t + 1) * P],
                        rhs=ax_q[0][:].bitcast(FP8X4),
                        rhs_scale=ax_q[1][:],
                        start=False,
                        stop=(t == t0 + per_bank - 1),
                    )
                bent = tile("bent", [P, BANK], F32, "bent", 3)
                nc.scalar.activation(out=bent[:], in_=bank[:], func=ACT.Tanh)
                last = c == CHUNKS - 1 and g == GROUPS - 1
                for t in range(t0, t0 + per_bank):
                    dst = y[:, t * CHUNK : (t + 1) * CHUNK]
                    src = bent[:, (t - t0) * CHUNK : (t - t0 + 1) * CHUNK]
                    factor = gains[:, g * PACK + t : g * PACK + t + 1]
                    if last:
                        nc.vector.tensor_scalar(out=dst, in0=src, scalar1=factor, scalar2=None, op0=ALU.mult)
                    else:
                        nc.scalar.activation(out=dst, in_=src, func=ACT.Copy, scale=factor)
                rows = out_0[g * PASS : (g + 1) * PASS, c * CHUNK : (c + 1) * CHUNK].rearrange("(p t) m -> p t m", t=PACK)
                planes = y[:].rearrange("p (t m) -> p t m", t=PACK)
                if last:
                    nc.sync.dma_start(out=rows[:, t0 : t0 + per_bank, :], in_=planes[:, t0 : t0 + per_bank, :])
            if not last:
                nc.sync.dma_start(out=rows, in_=planes)
            return y

        def round_y(y):
            y_bf = tile("y_bf", [P, PACK * CHUNK], BF16, "y_bf", 2)
            dst, src = woven(y_bf, y)
            nc.vector.tensor_copy(out=dst, in_=src)
            return y_bf

        def planes_of_y(c, g, y_bf):
            cols = slice(c * CHUNK, (c + 1) * CHUNK)
            nc.vector.quantize_mx(
                out=y_codes[g][:, cols].bitcast(FP8X4),
                scales=y_scales[:, g * M + c * CHUNK : g * M + (c + 1) * CHUNK],
                in_=y_bf[:],
            )
            nc.sync.dma_start(
                out=out_1[g].rearrange("p m t -> p (m t)").bitcast(I32)[:, cols], in_=y_codes[g][:, cols].bitcast(I32)
            )

        ys = []
        for c in range(CHUNKS):
            x_q, ax_q = make_x(c)
            for g in range(GROUPS):
                ys.append((c, g, make_y(c, g, x_q, ax_q)))
        pending = None
        for c, g, y in ys:
            y_bf = round_y(y)
            if pending is not None:
                planes_of_y(*pending)
            pending = (c, g, y_bf)
        planes_of_y(*pending)
        for q in range(QUADS):
            queue = nc.scalar if q % 2 else nc.sync
            queue.dma_start(
                out=out_2[:, 4 * q : 4 * q + 4, :].bitcast(I32).rearrange("g r w -> r g w"),
                in_=y_scales[32 * q : 32 * q + 4, :].bitcast(I32).rearrange("r (g w) -> r g w", g=GROUPS),
            )
